import numpy as np
import ml_dtypes


def mxq(x, axis, fmt="e4m3"):
    dtype, down = {"e4m3": (ml_dtypes.float8_e4m3fn, 7), "e5m2": (ml_dtypes.float8_e5m2, 14)}[fmt]
    v = np.moveaxis(np.asarray(x, np.float32).astype(ml_dtypes.bfloat16).astype(np.float64), axis, -1)
    blocks = v.reshape(v.shape[:-1] + (-1, 32))
    amax = np.abs(blocks).max(-1, keepdims=True)
    byte = np.maximum(np.where(amax > 0, np.frexp(amax)[1] - 1 + 127, 0) - down, 1)
    scale = np.exp2(byte - 127.0)
    codes = (blocks / scale).astype(np.float32).astype(dtype).astype(np.float64)
    return np.moveaxis((codes * scale).reshape(v.shape), -1, axis)


WIDE = False


def mx_kscale(k):
    if not WIDE:
        return np.ones(k)
    levels = np.array([10, -10, 5, -5, 0])
    if k % 512:
        return np.exp2(np.random.permutation(np.resize(levels, k // 32))).repeat(32)
    a = np.empty((k // 512, 16))
    for p in range(k // 512):
        a[p, :8] = np.random.permutation(np.resize(levels, 8))
        for g in range(8):
            far = levels[np.abs(levels - a[p, g]) >= 10]
            a[p, g + 8] = far[np.random.randint(len(far))]
    return np.exp2(a.ravel()).repeat(32)


BF16 = ml_dtypes.bfloat16


def bf(x):
    return np.asarray(x, np.float32).astype(BF16)


def f64(x):
    return np.asarray(x).astype(np.float64)

def planes(Y):
    n, m = Y.shape
    b = f64(bf(Y)).reshape(n // 32, 32, m)
    amax = np.abs(b).max(1)
    byte = np.clip(np.where(amax > 0, np.frexp(amax)[1] - 1 + 127 - 7, 1), 1, 254)
    codes = (b * np.exp2(127.0 - byte)[:, None, :]).reshape(n, m).astype(np.float32).astype(ml_dtypes.float8_e4m3fn).view(np.uint8)
    words = codes.reshape(n // 512, 128, 4, m).transpose(0, 1, 3, 2)
    return np.ascontiguousarray(words), np.ascontiguousarray(byte.astype(np.uint8).reshape(n // 512, 16, m))


M, D, F, O = 1024, 1024, 1024, 1024


def mode_angle(w, r2):
    return w[None, :] / (1.0 + 0.25 * r2)


def mode_growth(r2):
    return np.exp(0.25 * (1.0 - r2))


def setup_inputs():
    s, t = mx_kscale(D), mx_kscale(F)
    return {
        "x": bf(np.random.standard_normal((M, D)) * s),
        "er": bf(np.random.standard_normal((D, F)) / np.sqrt(D) / s[:, None]),
        "ei": bf(np.random.standard_normal((D, F)) / np.sqrt(D) / s[:, None]),
        "w": bf(np.random.uniform(0.5, 2.5, F)),
        "g": bf((1.0 + 0.1 * np.random.standard_normal(F)) * t),
        "dr": bf(np.random.standard_normal((F, O)) / np.sqrt(F) / t[:, None]),
        "di": bf(np.random.standard_normal((F, O)) / np.sqrt(F) / t[:, None]),
    }


def core(x, er, ei, w, g, dr, di):
    xq = mxq(f64(x), 1, "e4m3")
    zr = xq @ mxq(f64(er), 0, "e4m3")
    zi = xq @ mxq(f64(ei), 0, "e4m3")
    r2 = zr * zr + zi * zi
    theta = mode_angle(f64(w), r2)
    rho = mode_growth(r2)
    a = rho * f64(g)[None, :]
    c = np.cos(theta)
    sn = np.sin(theta)
    ur = a * (c * zr - sn * zi)
    ui = a * (sn * zr + c * zi)
    return (mxq(ur, 1, "e4m3") @ mxq(f64(dr), 0, "e4m3")) + (mxq(ui, 1, "e4m3") @ mxq(f64(di), 0, "e4m3"))


def reference(x, er, ei, w, g, dr, di):
    R_out = core(x, er, ei, w, g, dr, di)
    words, scales = planes(R_out.T)
    return R_out, words, scales

@@ -1,0 +1,452 @@
+import math
+from contextlib import ExitStack
+
+import concourse.mybir as mybir
+from concourse.masks import make_identity
+
+F32 = mybir.dt.float32
+BF16 = mybir.dt.bfloat16
+U32 = mybir.dt.uint32
+I32 = mybir.dt.int32
+U8 = mybir.dt.uint8
+FP8X4 = mybir.dt.float8_e4m3fn_x4
+ACT = mybir.ActivationFunctionType
+ALU = mybir.AluOpType
+ET = mybir.EngineType
+
+P = 128
+N = 1024
+FLOPS = 4 * 2 * N * N * N
+GROUPS = [[0],[1,2,3],[4,5],[6,7]]
+MANUAL = "s"
+HEAD_S = [("ei",0),("ei",1)]
+ADD_V = [0,1,2]
+TH_V = [0,1,2]
+DQ_ENG = "vvvvvvvv"
+OUT_ENG = "ss"
+PL_ENG = "s"
+XT_ENG = "ssssssss"
+E_LATE = 1
+DQ_AT = 0
+X_EARLY = 8
+X_MID = 2
+X_BUFS = 4
+LAG_D = 3
+FLAT = []
+
+
+def tile_koopmancontinuousspectrumstep_x1_kernel(tc, x, er, ei, w, g, dr, di, out_0, out_1, out_2):
+    nc = tc.nc
+    with ExitStack() as ctx:
+        keep = ctx.enter_context(tc.tile_pool(name="keep", bufs=1))
+        work = ctx.enter_context(tc.tile_pool(name="work", bufs=2))
+        psum = ctx.enter_context(tc.psum_pool(name="psum", bufs=1))
+        if MANUAL == "all":
+            ctx.enter_context(tc.manual_schedule())
+        elif MANUAL == "s":
+            ctx.enter_context(tc.manual_schedule(engines={ET.Activation, ET.SP}))
+        else:
+            ctx.enter_context(tc.manual_schedule(engines={ET.Activation, ET.SP, ET.PE}))
+
+        wb = keep.tile([P, 2, 4], BF16, name="wb")
+        gb = keep.tile([P, 2, 4], BF16, name="gb")
+        nc.scalar.dma_start(out=wb[:], in_=w.rearrange("(h p t) -> p h t", h=2, t=4))
+        nc.scalar.dma_start(out=gb[:], in_=g.rearrange("(h p t) -> p h t", h=2, t=4))
+        ident = keep.tile([P, P], F32, name="ident")
+        make_identity(nc, ident[:])
+
+        x_sb = {}
+
+        def load_x(mt):
+            t = work.tile([P, N], BF16, name="x_sb", bufs=X_BUFS, align_bytes=64)
+            nc.sync.dma_start(out=t[:], in_=x[mt * P : mt * P + P, :])
+            x_sb[mt] = t
+
+        raws = {}
+
+        def load_w(key, src, kg, h):
+            t = work.tile([P, 4, 512], BF16, name="raw", bufs=6, align_bytes=64)
+            nc.sync.dma_start(out=t[:], in_=src[kg * 512 : kg * 512 + 512, h * 512 : h * 512 + 512].rearrange("(p j) f -> p j f", j=4))
+            raws[key, kg, h] = t
+
+        codes = {}
+        scales = {}
+        for key in ("er", "ei", "dr", "di", "x"):
+            codes[key] = keep.tile([P, 2, N], U32, name="c_" + key, align_bytes=64)
+            scales[key] = keep.tile([P, 2, N], U8, name="s_" + key, align_bytes=64)
+        grouped = {}
+
+        def interleave(eng, key, kg, h):
+            t = work.tile([P, 512, 4], BF16, name="grp", bufs=3, align_bytes=64)
+            grouped[key, kg, h] = t
+            raw = raws[key, kg, h]
+            if key in ("er", "ei"):
+                dst = t[:].rearrange("p (t m) j -> p t m j", t=4)
+                src = raw[:].rearrange("p j (m t) -> p t m j", t=4)
+            else:
+                dst = t[:]
+                src = raw[:].rearrange("p j o -> p o j")
+            if eng == "v":
+                nc.vector.tensor_copy(out=dst, in_=src)
+            elif eng == "s":
+                nc.scalar.copy(out=dst, in_=src)
+            else:
+                nc.gpsimd.tensor_scalar(out=dst, in0=src, scalar1=1.0, scalar2=1.0, op0=ALU.mult, op1=ALU.mult)
+
+        def quant_w(key, kg, h):
+            t = grouped[key, kg, h]
+            cols = slice(h * 512, h * 512 + 512)
+            nc.vector.quantize_mx(
+                out=codes[key][:, kg, cols].bitcast(FP8X4),
+                scales=scales[key][:, kg, cols],
+                in_=t[:].rearrange("p c j -> p (c j)"),
+            )
+
+        def sbank():
+            return psum.tile([P, 512], F32, name="sb", bufs=4)
+
+        def copy_out(eng, dst, src):
+            if eng == "s":
+                nc.scalar.copy(out=dst, in_=src)
+            else:
+                nc.vector.tensor_copy(out=dst, in_=src)
+
+        def word_transposes(words):
+            bank = sbank()
+            for q in range(4):
+                kg, u = q // 2, q % 2
+                nc.tensor.transpose(bank[:, q * P : q * P + P], words[:, 256 * kg + u : 256 * kg + 256 : 2], ident[:])
+            return bank
+
+        xg = {}
+
+        def x_turn(mt):
+            bank = word_transposes(x_sb[mt][:].bitcast(F32))
+            t = work.tile([P, 2, P, 4], BF16, name="xg", bufs=2, align_bytes=64)
+            copy_out(
+                XT_ENG[mt],
+                t[:].rearrange("p k m t -> p (k m t)").bitcast(F32).rearrange("p (k m u) -> p k m u", k=2, u=2),
+                bank[:].rearrange("p (k u m) -> p k m u", k=2, u=2),
+            )
+            xg[mt] = t
+
+        def x_quant(mt):
+            for kg in range(2):
+                cols = slice(mt * P, mt * P + P)
+                nc.vector.quantize_mx(
+                    out=codes["x"][:, kg, cols].bitcast(FP8X4),
+                    scales=scales["x"][:, kg, cols],
+                    in_=xg[mt][:, kg, :, :].rearrange("p m t -> p (m t)"),
+                )
+
+        def mm(out, a, acols, b, bcols, start, stop):
+            nc.tensor.matmul_mx(
+                out=out,
+                lhsT=a[0][:, acols].bitcast(FP8X4),
+                lhsT_scale=a[1][:, acols],
+                rhs=b[0][:, bcols].bitcast(FP8X4),
+                rhs_scale=b[1][:, bcols],
+                start=start,
+                stop=stop,
+            )
+
+        def op(key, kg):
+            return codes[key][:, kg, :], scales[key][:, kg, :]
+
+        ys = {}
+        rhos = {}
+        css = {}
+
+        def squares(r, j):
+            q, gg = r // 2, r % 2
+            if j == 0:
+                ys[r] = work.tile([P, 4, 256], F32, name="y", bufs=4)
+            sq = []
+            for key in ("er", "ei"):
+                bank = sbank()
+                for a in range(2):
+                    gt = gg * 4 + 2 * j + a
+                    for kg in range(2):
+                        mm(bank[:, a * 256 : a * 256 + 256], op(key, kg), slice(gt * P, gt * P + P),
+                           op("x", kg), slice(q * 256, q * 256 + 256), kg == 0, kg == 1)
+                t = work.tile([P, 512], F32, name="sq", bufs=4)
+                nc.scalar.activation(out=t[:], in_=bank[:], func=ACT.Square, scale=0.5)
+                sq.append(t)
+            dst = ys[r][:, 2 * j : 2 * j + 2, :].rearrange("p t m -> p (t m)")
+            eng = nc.vector if r in ADD_V else nc.gpsimd
+            eng.tensor_tensor(out=dst, in0=sq[0][:], in1=sq[1][:], op=ALU.add)
+
+        def exps(r):
+            rhos[r] = work.tile([P, 4, 256], F32, name="rho", bufs=5)
+            nc.scalar.activation(out=rhos[r][:], in_=ys[r][:], func=ACT.Exp, scale=-1.0, bias=0.25)
+            for t in range(4):
+                v = rhos[r][:, t, :]
+                nc.gpsimd.tensor_scalar(out=v, in0=v, scalar1=gf[:, r % 2, t : t + 1], scalar2=1.0, op0=ALU.mult, op1=ALU.mult)
+
+        thetas = {}
+
+        def rsq(r):
+            thetas[r] = work.tile([P, 4, 256], F32, name="th", bufs=3)
+            for t in range(4):
+                c = iw[:, r % 2, t : t + 1]
+                nc.scalar.activation(out=thetas[r][:, t, :], in_=ys[r][:, t, :], func=ACT.Abs_reciprocal_sqrt, scale=c, bias=c)
+            eng = nc.vector if r in TH_V else nc.gpsimd
+            eng.tensor_tensor(out=thetas[r][:], in0=thetas[r][:], in1=thetas[r][:], op=ALU.mult)
+
+        def sines(r, ml):
+            if r in FLAT:
+                src = thetas[r][:, :, ml * P : ml * P + P]
+            else:
+                bank = sbank()
+                for t in range(4):
+                    nc.tensor.transpose(bank[:, t * P : t * P + P], thetas[r][:, t, ml * P : ml * P + P], ident[:])
+                src = bank[:].rearrange("p (t m) -> p t m", t=4)
+            cs = work.tile([P, 2, 4, P], F32, name="cs", bufs=7)
+            nc.scalar.activation(out=cs[:, 0, :, :], in_=src, func=ACT.Sin, scale=-1.0, bias=math.pi / 2)
+            nc.scalar.activation(out=cs[:, 1, :, :], in_=src, func=ACT.Sin)
+            css[r, ml] = cs
+
+        def weigh(i):
+            r, ml, mt, gg = place(i)
+            if r in FLAT:
+                for k in range(2):
+                    v = css[r, ml][:, k, :, :]
+                    nc.vector.tensor_tensor(out=v, in0=v, in1=rhos[r][:, :, ml * P : ml * P + P], op=ALU.mult)
+
+        zb = {}
+        prod = {}
+        db = {}
+        ugs = {}
+        uqs = {}
+        obs = {}
+        obf = {}
+        planes_w = keep.tile([P, 2, N], U32, name="planes_w", align_bytes=64)
+        planes_s = keep.tile([P, 2, N], U8, name="planes_s", align_bytes=64)
+
+        def place(i):
+            r, ml = i // 2, i % 2
+            return r, ml, 2 * (r // 2) + ml, r % 2
+
+        def z2(i):
+            r, ml, mt, gg = place(i)
+            for key, nm in (("er", "zr"), ("ei", "zi")):
+                bank = psum.tile([P, 512], F32, name=nm, bufs=1)
+                if r in FLAT:
+                    for t in range(4):
+                        for kg in range(2):
+                            gt = 4 * gg + t
+                            mm(bank[:, t * P : t * P + P], op(key, kg), slice(gt * P, gt * P + P), op("x", kg), slice(mt * P, mt * P + P), kg == 0, kg == 1)
+                else:
+                    for kg in range(2):
+                        mm(bank[:], op("x", kg), slice(mt * P, mt * P + P), op(key, kg), slice(gg * 512, gg * 512 + 512), kg == 0, kg == 1)
+                zb[i, key] = bank
+
+        def products(i):
+            r, ml, mt, gg = place(i)
+            cs = css[r, ml][:].rearrange("p k t m -> p k (t m)")
+            zr, zi = zb[i, "er"], zb[i, "ei"]
+            t = [work.tile([P, 512], F32, name="pr" + str(k), bufs=2) for k in range(4)]
+            nc.vector.tensor_tensor(out=t[0][:], in0=zr[:], in1=cs[:, 0, :], op=ALU.mult)
+            nc.vector.tensor_tensor(out=t[1][:], in0=zr[:], in1=cs[:, 1, :], op=ALU.mult)
+            nc.vector.scalar_tensor_tensor(out=t[2][:], in0=zi[:], scalar=-1.0, in1=cs[:, 1, :], op0=ALU.mult, op1=ALU.mult)
+            nc.vector.tensor_tensor(out=t[3][:], in0=zi[:], in1=cs[:, 0, :], op=ALU.mult)
+            prod[i] = t
+
+        def turn(i):
+            t = prod[i]
+            if place(i)[0] in FLAT:
+                return
+            for nm, pair in (("dre", (t[0], t[2])), ("dim", (t[1], t[3]))):
+                bank = psum.tile([P, 512], F32, name=nm, bufs=1)
+                for q in range(4):
+                    c = slice(q * P, q * P + P)
+                    for k in range(2):
+                        nc.tensor.matmul(bank[:, c], lhsT=pair[k][:, c], rhs=ident[:], start=k == 0, stop=k == 1, is_transpose=True)
+                db[i, nm] = bank
+
+        def u(i):
+            r, ml, mt, gg = place(i)
+            ug = work.tile([P, 2, P, 4], BF16, name="ug", bufs=3, align_bytes=64)
+            rho = rhos[r][:, :, ml * P : ml * P + P].rearrange("p t m -> p m t")
+            if r in FLAT:
+                t = [a[:].rearrange("p (t m) -> p m t", t=4) for a in prod[i]]
+                for k in range(2):
+                    nc.vector.tensor_tensor(out=ug[:, k, :, :], in0=t[k], in1=t[k + 2], op=ALU.add)
+                ugs[i] = ug
+                return
+            for k, nm in enumerate(("dre", "dim")):
+                nc.vector.tensor_tensor(out=ug[:, k, :, :], in0=db[i, nm][:].rearrange("p (t m) -> p m t", t=4), in1=rho, op=ALU.mult)
+            ugs[i] = ug
+
+        def uquant(i):
+            c = work.tile([P, 256], U32, name="uq", bufs=6, align_bytes=64)
+            s = work.tile([P, 256], U8, name="us", bufs=6, align_bytes=64)
+            nc.vector.quantize_mx(out=c[:].bitcast(FP8X4), scales=s[:], in_=ugs[i][:].rearrange("p k m t -> p (k m t)"))
+            r, ml, mt, gg = place(i)
+            uqs[mt, gg] = (c[:], s[:])
+
+        def decode(mt):
+            o = work.tile([P, N], F32, name="o", bufs=2)
+            for oh in range(2):
+                bank = sbank()
+                n = 0
+                for gg in range(2):
+                    for k, key in enumerate(("dr", "di")):
+                        mm(bank[:], uqs[mt, gg], slice(k * P, k * P + P), op(key, gg), slice(oh * 512, oh * 512 + 512), n == 0, n == 3)
+                        n += 1
+                copy_out(OUT_ENG[oh], o[:, oh * 512 : oh * 512 + 512], bank[:])
+            nc.sync.dma_start(out=out_0[mt * P : mt * P + P, :], in_=o[:])
+            obs[mt] = o
+
+        def cast(mt):
+            t = work.tile([P, N], BF16, name="obf", bufs=2, align_bytes=64)
+            nc.vector.tensor_copy(out=t[:], in_=obs[mt][:])
+            obf[mt] = t
+
+        pgs = {}
+
+        def planes_turn(mt):
+            bank = word_transposes(obf[mt][:].bitcast(F32))
+            t = work.tile([P, 2, P, 4], BF16, name="pg", bufs=2, align_bytes=64)
+            copy_out(
+                PL_ENG,
+                t[:].rearrange("p k m t -> p (k m t)").bitcast(F32).rearrange("p (k m u) -> p k m u", k=2, u=2),
+                bank[:].rearrange("p (k u m) -> p k m u", k=2, u=2),
+            )
+            pgs[mt] = t
+
+        def planes_quant(mt):
+            cols = slice(mt * P, mt * P + P)
+            for og in range(2):
+                nc.vector.quantize_mx(
+                    out=planes_w[:, og, cols].bitcast(FP8X4),
+                    scales=planes_s[:, og, cols],
+                    in_=pgs[mt][:, og, :, :].rearrange("p m t -> p (m t)"),
+                )
+            nc.sync.dma_start(
+                out=out_1.bitcast(I32).rearrange("g p m o -> p g (m o)")[:, :, cols],
+                in_=planes_w[:, :, cols].bitcast(I32),
+            )
+
+        load_x(0)
+        load_x(1)
+        for h in range(2):
+            for kg in range(2):
+                for key, src in (("er", er), ("ei", ei)):
+                    load_w(key, src, kg, h)
+        for mt in range(2, X_EARLY):
+            load_x(mt)
+        dq = [(key, kg, h) for h in range(2) for kg in range(2) for key in ("dr", "di")]
+        for key, kg, h in dq[:2]:
+            load_w(key, dr if key == "dr" else di, kg, h)
+        for key, kg, h in dq[2:]:
+            load_w(key, dr if key == "dr" else di, kg, h)
+        for mt in range(X_EARLY, 8):
+            load_x(mt)
+
+        x_turn(0)
+        x_turn(1)
+        iw = keep.tile([P, 2, 4], F32, name="iw")
+        gf = keep.tile([P, 2, 4], F32, name="gf")
+        nc.vector.tensor_copy(out=gf[:], in_=gb[:])
+        nc.vector.reciprocal(out=iw[:], in_=wb[:])
+        head = [(key, kg, 0) for kg in range(2) for key in ("er", "ei")]
+        head2 = [(key, kg, 1) for kg in range(2) for key in ("er", "ei")]
+
+        def eng_of(it):
+            return "s" if (it[0], it[1] + 2 * it[2]) in HEAD_S else "v"
+
+        x_quant(0)
+        x_quant(1)
+        interleave(eng_of(head[0]), *head[0])
+        for a in range(1, 4):
+            interleave(eng_of(head[a]), *head[a])
+            quant_w(*head[a - 1])
+        quant_w(*head[3])
+
+        todo_v = []
+        for a in range(4):
+            todo_v.append(lambda a=a: interleave(eng_of(head2[a]), *head2[a]))
+            if a:
+                todo_v.append(lambda a=a: quant_w(*head2[a - 1]))
+        todo_v.append(lambda: quant_w(*head2[3]))
+
+        squares(0, 0)
+        squares(0, 1)
+        rsq(0)
+        for fn in todo_v:
+            fn()
+        for mt in range(2, X_MID):
+            x_turn(mt)
+            x_quant(mt)
+        sines(0, 0)
+        sines(0, 1)
+        for mt in range(X_MID, X_EARLY):
+            x_turn(mt)
+            x_quant(mt)
+        if not E_LATE:
+            exps(0)
+
+        n_chunks = 16
+        dq_g = [lambda it=it, e=DQ_ENG[k]: interleave(e, *it) for k, it in enumerate(dq)]
+        dq_v = [lambda it=it: quant_w(*it) for it in dq]
+        for k in range(DQ_AT):
+            dq_g.pop(0)()
+        z2(0)
+        for k, grp in enumerate(GROUPS):
+            mine = [i for r in grp for i in (2 * r, 2 * r + 1)]
+            nxt = []
+            if k + 1 < len(GROUPS):
+                ng = GROUPS[k + 1]
+                for r in ng:
+                    if r % 2 == 0:
+                        for mt in range(max(r, X_EARLY), r + 2):
+                            nxt.append((256, lambda mt=mt: (x_turn(mt), x_quant(mt))))
+                    for j in range(2):
+                        nxt.append((512, lambda r=r, j=j: squares(r, j)))
+                for r in ([0] if k == 0 and E_LATE else []) + ng:
+                    nxt.append((1024, lambda r=r: exps(r)))
+                for r in ng:
+                    nxt.append((1024, lambda r=r: rsq(r)))
+                for r in ng:
+                    for ml in range(2):
+                        nxt.append((1024, lambda r=r, ml=ml: sines(r, ml)))
+            total = sum(c for c, _ in nxt)
+            done = 0
+            for n, i in enumerate(mine):
+                weigh(i)
+                products(i)
+                if i + 1 < n_chunks:
+                    nz = lambda i=i: z2(i + 1)
+                    nz()
+                turn(i)
+                while nxt and done < total * (n + 1) / len(mine) - 1:
+                    c, fn = nxt.pop(0)
+                    done += c
+                    fn()
+                if i >= 1:
+                    u(i - 1)
+                if i >= 2:
+                    uquant(i - 2)
+                for _ in range(2):
+                    if dq_g:
+                        dq_g.pop(0)()
+                    if dq_v and len(dq_g) < len(dq_v) - 1 or dq_v and not dq_g:
+                        dq_v.pop(0)()
+                for lag, fn in ((LAG_D, decode), (LAG_D + 1, cast), (LAG_D + 2, planes_turn), (LAG_D + 3, planes_quant)):
+                    a = i - lag
+                    if a >= 0 and (a // 2) % 2 == 1:
+                        fn(place(a)[2])
+        u(15)
+        uquant(14)
+        uquant(15)
+        for a in range(16, 16 + LAG_D + 3):
+            for lag, fn in ((LAG_D, decode), (LAG_D + 1, cast), (LAG_D + 2, planes_turn), (LAG_D + 3, planes_quant)):
+                c = a - lag
+                if 0 <= c < 16 and (c // 2) % 2 == 1:
+                    fn(place(c)[2])
+        for q in range(4):
+            nc.sync.dma_start(
+                out=out_2[:, 4 * q : 4 * q + 4, :].rearrange("g r m -> r g m").bitcast(I32),
+                in_=planes_s[32 * q : 32 * q + 4, :, :].bitcast(I32),
+            )

@@ -20,8 +20,8 @@ FLOPS = 4 * 2 * N * N * N
 GROUPS = [[0],[1,2,3],[4,5],[6,7]]
 MANUAL = "s"
 HEAD_S = [("ei",0),("ei",1)]
-ADD_V = [0,1,2]
-TH_V = [0,1,2]
+ADD_V = [0,1,2,3,4,5,6,7]
+TH_V = [0,1,2,3]
 DQ_ENG = "vvvvvvvv"
 OUT_ENG = "ss"
 PL_ENG = "s"
@@ -33,6 +33,8 @@ X_MID = 2
 X_BUFS = 4
 LAG_D = 3
 FLAT = []
+TH_S = [4,5,6,7]
+RG_V = 1
 
 
 def tile_koopmancontinuousspectrumstep_x1_kernel(tc, x, er, ei, w, g, dr, di, out_0, out_1, out_2):
@@ -181,7 +183,10 @@ def tile_koopmancontinuousspectrumstep_x1_kernel(tc, x, er, ei, w, g, dr, di, ou
             nc.scalar.activation(out=rhos[r][:], in_=ys[r][:], func=ACT.Exp, scale=-1.0, bias=0.25)
             for t in range(4):
                 v = rhos[r][:, t, :]
-                nc.gpsimd.tensor_scalar(out=v, in0=v, scalar1=gf[:, r % 2, t : t + 1], scalar2=1.0, op0=ALU.mult, op1=ALU.mult)
+                if RG_V:
+                    nc.vector.tensor_scalar(out=v, in0=v, scalar1=gf[:, r % 2, t : t + 1], scalar2=None, op0=ALU.mult)
+                else:
+                    nc.gpsimd.tensor_scalar(out=v, in0=v, scalar1=gf[:, r % 2, t : t + 1], scalar2=1.0, op0=ALU.mult, op1=ALU.mult)
 
         thetas = {}
 
@@ -190,6 +195,9 @@ def tile_koopmancontinuousspectrumstep_x1_kernel(tc, x, er, ei, w, g, dr, di, ou
             for t in range(4):
                 c = iw[:, r % 2, t : t + 1]
                 nc.scalar.activation(out=thetas[r][:, t, :], in_=ys[r][:, t, :], func=ACT.Abs_reciprocal_sqrt, scale=c, bias=c)
+            if r in TH_S:
+                nc.scalar.activation(out=thetas[r][:], in_=thetas[r][:], func=ACT.Square)
+                return
             eng = nc.vector if r in TH_V else nc.gpsimd
             eng.tensor_tensor(out=thetas[r][:], in0=thetas[r][:], in1=thetas[r][:], op=ALU.mult)
 

@@ -35,6 +35,9 @@ LAG_D = 3
 FLAT = []
 TH_S = [4,5,6,7]
 RG_V = 1
+EIL = 1
+DIL = 1
+UIL = 1
 
 
 def tile_koopmancontinuousspectrumstep_x1_kernel(tc, x, er, ei, w, g, dr, di, out_0, out_1, out_2):
@@ -83,8 +86,15 @@ def tile_koopmancontinuousspectrumstep_x1_kernel(tc, x, er, ei, w, g, dr, di, ou
             grouped[key, kg, h] = t
             raw = raws[key, kg, h]
             if key in ("er", "ei"):
-                dst = t[:].rearrange("p (t m) j -> p t m j", t=4)
-                src = raw[:].rearrange("p j (m t) -> p t m j", t=4)
+                if EIL:
+                    dst = t[:].rearrange("p (t a b) j -> p a j b t", t=4, b=2)
+                    src = raw[:].rearrange("p j (a b t) -> p a j b t", t=4, b=2)
+                else:
+                    dst = t[:].rearrange("p (t m) j -> p t m j", t=4)
+                    src = raw[:].rearrange("p j (m t) -> p t m j", t=4)
+            elif DIL:
+                dst = t[:].rearrange("p (c i) j -> p c j i", i=4)
+                src = raw[:].rearrange("p j (c i) -> p c j i", i=4)
             else:
                 dst = t[:]
                 src = raw[:].rearrange("p j o -> p o j")
@@ -283,7 +293,15 @@ def tile_koopmancontinuousspectrumstep_x1_kernel(tc, x, er, ei, w, g, dr, di, ou
                 ugs[i] = ug
                 return
             for k, nm in enumerate(("dre", "dim")):
-                nc.vector.tensor_tensor(out=ug[:, k, :, :], in0=db[i, nm][:].rearrange("p (t m) -> p m t", t=4), in1=rho, op=ALU.mult)
+                if UIL:
+                    nc.vector.tensor_tensor(
+                        out=ug[:, k, :, :].rearrange("p (c i) t -> p c t i", i=4),
+                        in0=db[i, nm][:].rearrange("p (t c i) -> p c t i", t=4, i=4),
+                        in1=rhos[r][:, :, ml * P : ml * P + P].rearrange("p t (c i) -> p c t i", i=4),
+                        op=ALU.mult,
+                    )
+                else:
+                    nc.vector.tensor_tensor(out=ug[:, k, :, :], in0=db[i, nm][:].rearrange("p (t m) -> p m t", t=4), in1=rho, op=ALU.mult)
             ugs[i] = ug
 
         def uquant(i):

import math
from contextlib import ExitStack

import concourse.mybir as mybir
from concourse.masks import make_identity

F32 = mybir.dt.float32
BF16 = mybir.dt.bfloat16
U32 = mybir.dt.uint32
I32 = mybir.dt.int32
U8 = mybir.dt.uint8
FP8X4 = mybir.dt.float8_e4m3fn_x4
ACT = mybir.ActivationFunctionType
ALU = mybir.AluOpType
ET = mybir.EngineType

P = 128
N = 1024
FLOPS = 4 * 2 * N * N * N
GROUPS = [[0],[1,2,3],[4,5],[6,7]]
MANUAL = "s"
HEAD_S = [("ei",0),("ei",1)]
ADD_V = [0,1,2,3,4,5,6,7]
TH_V = [0,1,2,3]
DQ_ENG = "vvvvvvvv"
OUT_ENG = "ss"
PL_ENG = "s"
XT_ENG = "ssssssss"
E_LATE = 1
DQ_AT = 0
X_EARLY = 8
X_MID = 2
X_BUFS = 4
LAG_D = 3
FLAT = []
TH_S = [4,5,6,7]
RG_V = 1
EIL = 1
DIL = 1
UIL = 1


def tile_koopmancontinuousspectrumstep_x1_kernel(tc, x, er, ei, w, g, dr, di, out_0, out_1, out_2):
    nc = tc.nc
    with ExitStack() as ctx:
        keep = ctx.enter_context(tc.tile_pool(name="keep", bufs=1))
        work = ctx.enter_context(tc.tile_pool(name="work", bufs=2))
        psum = ctx.enter_context(tc.psum_pool(name="psum", bufs=1))
        if MANUAL == "all":
            ctx.enter_context(tc.manual_schedule())
        elif MANUAL == "s":
            ctx.enter_context(tc.manual_schedule(engines={ET.Activation, ET.SP}))
        else:
            ctx.enter_context(tc.manual_schedule(engines={ET.Activation, ET.SP, ET.PE}))

        wb = keep.tile([P, 2, 4], BF16, name="wb")
        gb = keep.tile([P, 2, 4], BF16, name="gb")
        nc.scalar.dma_start(out=wb[:], in_=w.rearrange("(h p t) -> p h t", h=2, t=4))
        nc.scalar.dma_start(out=gb[:], in_=g.rearrange("(h p t) -> p h t", h=2, t=4))
        ident = keep.tile([P, P], F32, name="ident")
        make_identity(nc, ident[:])

        x_sb = {}

        def load_x(mt):
            t = work.tile([P, N], BF16, name="x_sb", bufs=X_BUFS, align_bytes=64)
            nc.sync.dma_start(out=t[:], in_=x[mt * P : mt * P + P, :])
            x_sb[mt] = t

        raws = {}

        def load_w(key, src, kg, h):
            t = work.tile([P, 4, 512], BF16, name="raw", bufs=6, align_bytes=64)
            nc.sync.dma_start(out=t[:], in_=src[kg * 512 : kg * 512 + 512, h * 512 : h * 512 + 512].rearrange("(p j) f -> p j f", j=4))
            raws[key, kg, h] = t

        codes = {}
        scales = {}
        for key in ("er", "ei", "dr", "di", "x"):
            codes[key] = keep.tile([P, 2, N], U32, name="c_" + key, align_bytes=64)
            scales[key] = keep.tile([P, 2, N], U8, name="s_" + key, align_bytes=64)
        grouped = {}

        def interleave(eng, key, kg, h):
            t = work.tile([P, 512, 4], BF16, name="grp", bufs=3, align_bytes=64)
            grouped[key, kg, h] = t
            raw = raws[key, kg, h]
            if key in ("er", "ei"):
                if EIL:
                    dst = t[:].rearrange("p (t a b) j -> p a j b t", t=4, b=2)
                    src = raw[:].rearrange("p j (a b t) -> p a j b t", t=4, b=2)
                else:
                    dst = t[:].rearrange("p (t m) j -> p t m j", t=4)
                    src = raw[:].rearrange("p j (m t) -> p t m j", t=4)
            elif DIL:
                dst = t[:].rearrange("p (c i) j -> p c j i", i=4)
                src = raw[:].rearrange("p j (c i) -> p c j i", i=4)
            else:
                dst = t[:]
                src = raw[:].rearrange("p j o -> p o j")
            if eng == "v":
                nc.vector.tensor_copy(out=dst, in_=src)
            elif eng == "s":
                nc.scalar.copy(out=dst, in_=src)
            else:
                nc.gpsimd.tensor_scalar(out=dst, in0=src, scalar1=1.0, scalar2=1.0, op0=ALU.mult, op1=ALU.mult)

        def quant_w(key, kg, h):
            t = grouped[key, kg, h]
            cols = slice(h * 512, h * 512 + 512)
            nc.vector.quantize_mx(
                out=codes[key][:, kg, cols].bitcast(FP8X4),
                scales=scales[key][:, kg, cols],
                in_=t[:].rearrange("p c j -> p (c j)"),
            )

        def sbank():
            return psum.tile([P, 512], F32, name="sb", bufs=4)

        def copy_out(eng, dst, src):
            if eng == "s":
                nc.scalar.copy(out=dst, in_=src)
            else:
                nc.vector.tensor_copy(out=dst, in_=src)

        def word_transposes(words):
            bank = sbank()
            for q in range(4):
                kg, u = q // 2, q % 2
                nc.tensor.transpose(bank[:, q * P : q * P + P], words[:, 256 * kg + u : 256 * kg + 256 : 2], ident[:])
            return bank

        xg = {}

        def x_turn(mt):
            bank = word_transposes(x_sb[mt][:].bitcast(F32))
            t = work.tile([P, 2, P, 4], BF16, name="xg", bufs=2, align_bytes=64)
            copy_out(
                XT_ENG[mt],
                t[:].rearrange("p k m t -> p (k m t)").bitcast(F32).rearrange("p (k m u) -> p k m u", k=2, u=2),
                bank[:].rearrange("p (k u m) -> p k m u", k=2, u=2),
            )
            xg[mt] = t

        def x_quant(mt):
            for kg in range(2):
                cols = slice(mt * P, mt * P + P)
                nc.vector.quantize_mx(
                    out=codes["x"][:, kg, cols].bitcast(FP8X4),
                    scales=scales["x"][:, kg, cols],
                    in_=xg[mt][:, kg, :, :].rearrange("p m t -> p (m t)"),
                )

        def mm(out, a, acols, b, bcols, start, stop):
            nc.tensor.matmul_mx(
                out=out,
                lhsT=a[0][:, acols].bitcast(FP8X4),
                lhsT_scale=a[1][:, acols],
                rhs=b[0][:, bcols].bitcast(FP8X4),
                rhs_scale=b[1][:, bcols],
                start=start,
                stop=stop,
            )

        def op(key, kg):
            return codes[key][:, kg, :], scales[key][:, kg, :]

        ys = {}
        rhos = {}
        css = {}

        def squares(r, j):
            q, gg = r // 2, r % 2
            if j == 0:
                ys[r] = work.tile([P, 4, 256], F32, name="y", bufs=4)
            sq = []
            for key in ("er", "ei"):
                bank = sbank()
                for a in range(2):
                    gt = gg * 4 + 2 * j + a
                    for kg in range(2):
                        mm(bank[:, a * 256 : a * 256 + 256], op(key, kg), slice(gt * P, gt * P + P),
                           op("x", kg), slice(q * 256, q * 256 + 256), kg == 0, kg == 1)
                t = work.tile([P, 512], F32, name="sq", bufs=4)
                nc.scalar.activation(out=t[:], in_=bank[:], func=ACT.Square, scale=0.5)
                sq.append(t)
            dst = ys[r][:, 2 * j : 2 * j + 2, :].rearrange("p t m -> p (t m)")
            eng = nc.vector if r in ADD_V else nc.gpsimd
            eng.tensor_tensor(out=dst, in0=sq[0][:], in1=sq[1][:], op=ALU.add)

        def exps(r):
            rhos[r] = work.tile([P, 4, 256], F32, name="rho", bufs=5)
            nc.scalar.activation(out=rhos[r][:], in_=ys[r][:], func=ACT.Exp, scale=-1.0, bias=0.25)
            for t in range(4):
                v = rhos[r][:, t, :]
                if RG_V:
                    nc.vector.tensor_scalar(out=v, in0=v, scalar1=gf[:, r % 2, t : t + 1], scalar2=None, op0=ALU.mult)
                else:
                    nc.gpsimd.tensor_scalar(out=v, in0=v, scalar1=gf[:, r % 2, t : t + 1], scalar2=1.0, op0=ALU.mult, op1=ALU.mult)

        thetas = {}

        def rsq(r):
            thetas[r] = work.tile([P, 4, 256], F32, name="th", bufs=3)
            for t in range(4):
                c = iw[:, r % 2, t : t + 1]
                nc.scalar.activation(out=thetas[r][:, t, :], in_=ys[r][:, t, :], func=ACT.Abs_reciprocal_sqrt, scale=c, bias=c)
            if r in TH_S:
                nc.scalar.activation(out=thetas[r][:], in_=thetas[r][:], func=ACT.Square)
                return
            eng = nc.vector if r in TH_V else nc.gpsimd
            eng.tensor_tensor(out=thetas[r][:], in0=thetas[r][:], in1=thetas[r][:], op=ALU.mult)

        def sines(r, ml):
            if r in FLAT:
                src = thetas[r][:, :, ml * P : ml * P + P]
            else:
                bank = sbank()
                for t in range(4):
                    nc.tensor.transpose(bank[:, t * P : t * P + P], thetas[r][:, t, ml * P : ml * P + P], ident[:])
                src = bank[:].rearrange("p (t m) -> p t m", t=4)
            cs = work.tile([P, 2, 4, P], F32, name="cs", bufs=7)
            nc.scalar.activation(out=cs[:, 0, :, :], in_=src, func=ACT.Sin, scale=-1.0, bias=math.pi / 2)
            nc.scalar.activation(out=cs[:, 1, :, :], in_=src, func=ACT.Sin)
            css[r, ml] = cs

        def weigh(i):
            r, ml, mt, gg = place(i)
            if r in FLAT:
                for k in range(2):
                    v = css[r, ml][:, k, :, :]
                    nc.vector.tensor_tensor(out=v, in0=v, in1=rhos[r][:, :, ml * P : ml * P + P], op=ALU.mult)

        zb = {}
        prod = {}
        db = {}
        ugs = {}
        uqs = {}
        obs = {}
        obf = {}
        planes_w = keep.tile([P, 2, N], U32, name="planes_w", align_bytes=64)
        planes_s = keep.tile([P, 2, N], U8, name="planes_s", align_bytes=64)

        def place(i):
            r, ml = i // 2, i % 2
            return r, ml, 2 * (r // 2) + ml, r % 2

        def z2(i):
            r, ml, mt, gg = place(i)
            for key, nm in (("er", "zr"), ("ei", "zi")):
                bank = psum.tile([P, 512], F32, name=nm, bufs=1)
                if r in FLAT:
                    for t in range(4):
                        for kg in range(2):
                            gt = 4 * gg + t
                            mm(bank[:, t * P : t * P + P], op(key, kg), slice(gt * P, gt * P + P), op("x", kg), slice(mt * P, mt * P + P), kg == 0, kg == 1)
                else:
                    for kg in range(2):
                        mm(bank[:], op("x", kg), slice(mt * P, mt * P + P), op(key, kg), slice(gg * 512, gg * 512 + 512), kg == 0, kg == 1)
                zb[i, key] = bank

        def products(i):
            r, ml, mt, gg = place(i)
            cs = css[r, ml][:].rearrange("p k t m -> p k (t m)")
            zr, zi = zb[i, "er"], zb[i, "ei"]
            t = [work.tile([P, 512], F32, name="pr" + str(k), bufs=2) for k in range(4)]
            nc.vector.tensor_tensor(out=t[0][:], in0=zr[:], in1=cs[:, 0, :], op=ALU.mult)
            nc.vector.tensor_tensor(out=t[1][:], in0=zr[:], in1=cs[:, 1, :], op=ALU.mult)
            nc.vector.scalar_tensor_tensor(out=t[2][:], in0=zi[:], scalar=-1.0, in1=cs[:, 1, :], op0=ALU.mult, op1=ALU.mult)
            nc.vector.tensor_tensor(out=t[3][:], in0=zi[:], in1=cs[:, 0, :], op=ALU.mult)
            prod[i] = t

        def turn(i):
            t = prod[i]
            if place(i)[0] in FLAT:
                return
            for nm, pair in (("dre", (t[0], t[2])), ("dim", (t[1], t[3]))):
                bank = psum.tile([P, 512], F32, name=nm, bufs=1)
                for q in range(4):
                    c = slice(q * P, q * P + P)
                    for k in range(2):
                        nc.tensor.matmul(bank[:, c], lhsT=pair[k][:, c], rhs=ident[:], start=k == 0, stop=k == 1, is_transpose=True)
                db[i, nm] = bank

        def u(i):
            r, ml, mt, gg = place(i)
            ug = work.tile([P, 2, P, 4], BF16, name="ug", bufs=3, align_bytes=64)
            rho = rhos[r][:, :, ml * P : ml * P + P].rearrange("p t m -> p m t")
            if r in FLAT:
                t = [a[:].rearrange("p (t m) -> p m t", t=4) for a in prod[i]]
                for k in range(2):
                    nc.vector.tensor_tensor(out=ug[:, k, :, :], in0=t[k], in1=t[k + 2], op=ALU.add)
                ugs[i] = ug
                return
            for k, nm in enumerate(("dre", "dim")):
                if UIL:
                    nc.vector.tensor_tensor(
                        out=ug[:, k, :, :].rearrange("p (c i) t -> p c t i", i=4),
                        in0=db[i, nm][:].rearrange("p (t c i) -> p c t i", t=4, i=4),
                        in1=rhos[r][:, :, ml * P : ml * P + P].rearrange("p t (c i) -> p c t i", i=4),
                        op=ALU.mult,
                    )
                else:
                    nc.vector.tensor_tensor(out=ug[:, k, :, :], in0=db[i, nm][:].rearrange("p (t m) -> p m t", t=4), in1=rho, op=ALU.mult)
            ugs[i] = ug

        def uquant(i):
            c = work.tile([P, 256], U32, name="uq", bufs=6, align_bytes=64)
            s = work.tile([P, 256], U8, name="us", bufs=6, align_bytes=64)
            nc.vector.quantize_mx(out=c[:].bitcast(FP8X4), scales=s[:], in_=ugs[i][:].rearrange("p k m t -> p (k m t)"))
            r, ml, mt, gg = place(i)
            uqs[mt, gg] = (c[:], s[:])

        def decode(mt):
            o = work.tile([P, N], F32, name="o", bufs=2)
            for oh in range(2):
                bank = sbank()
                n = 0
                for gg in range(2):
                    for k, key in enumerate(("dr", "di")):
                        mm(bank[:], uqs[mt, gg], slice(k * P, k * P + P), op(key, gg), slice(oh * 512, oh * 512 + 512), n == 0, n == 3)
                        n += 1
                copy_out(OUT_ENG[oh], o[:, oh * 512 : oh * 512 + 512], bank[:])
            nc.sync.dma_start(out=out_0[mt * P : mt * P + P, :], in_=o[:])
            obs[mt] = o

        def cast(mt):
            t = work.tile([P, N], BF16, name="obf", bufs=2, align_bytes=64)
            nc.vector.tensor_copy(out=t[:], in_=obs[mt][:])
            obf[mt] = t

        pgs = {}

        def planes_turn(mt):
            bank = word_transposes(obf[mt][:].bitcast(F32))
            t = work.tile([P, 2, P, 4], BF16, name="pg", bufs=2, align_bytes=64)
            copy_out(
                PL_ENG,
                t[:].rearrange("p k m t -> p (k m t)").bitcast(F32).rearrange("p (k m u) -> p k m u", k=2, u=2),
                bank[:].rearrange("p (k u m) -> p k m u", k=2, u=2),
            )
            pgs[mt] = t

        def planes_quant(mt):
            cols = slice(mt * P, mt * P + P)
            for og in range(2):
                nc.vector.quantize_mx(
                    out=planes_w[:, og, cols].bitcast(FP8X4),
                    scales=planes_s[:, og, cols],
                    in_=pgs[mt][:, og, :, :].rearrange("p m t -> p (m t)"),
                )
            nc.sync.dma_start(
                out=out_1.bitcast(I32).rearrange("g p m o -> p g (m o)")[:, :, cols],
                in_=planes_w[:, :, cols].bitcast(I32),
            )

        load_x(0)
        load_x(1)
        for h in range(2):
            for kg in range(2):
                for key, src in (("er", er), ("ei", ei)):
                    load_w(key, src, kg, h)
        for mt in range(2, X_EARLY):
            load_x(mt)
        dq = [(key, kg, h) for h in range(2) for kg in range(2) for key in ("dr", "di")]
        for key, kg, h in dq[:2]:
            load_w(key, dr if key == "dr" else di, kg, h)
        for key, kg, h in dq[2:]:
            load_w(key, dr if key == "dr" else di, kg, h)
        for mt in range(X_EARLY, 8):
            load_x(mt)

        x_turn(0)
        x_turn(1)
        iw = keep.tile([P, 2, 4], F32, name="iw")
        gf = keep.tile([P, 2, 4], F32, name="gf")
        nc.vector.tensor_copy(out=gf[:], in_=gb[:])
        nc.vector.reciprocal(out=iw[:], in_=wb[:])
        head = [(key, kg, 0) for kg in range(2) for key in ("er", "ei")]
        head2 = [(key, kg, 1) for kg in range(2) for key in ("er", "ei")]

        def eng_of(it):
            return "s" if (it[0], it[1] + 2 * it[2]) in HEAD_S else "v"

        x_quant(0)
        x_quant(1)
        interleave(eng_of(head[0]), *head[0])
        for a in range(1, 4):
            interleave(eng_of(head[a]), *head[a])
            quant_w(*head[a - 1])
        quant_w(*head[3])

        todo_v = []
        for a in range(4):
            todo_v.append(lambda a=a: interleave(eng_of(head2[a]), *head2[a]))
            if a:
                todo_v.append(lambda a=a: quant_w(*head2[a - 1]))
        todo_v.append(lambda: quant_w(*head2[3]))

        squares(0, 0)
        squares(0, 1)
        rsq(0)
        for fn in todo_v:
            fn()
        for mt in range(2, X_MID):
            x_turn(mt)
            x_quant(mt)
        sines(0, 0)
        sines(0, 1)
        for mt in range(X_MID, X_EARLY):
            x_turn(mt)
            x_quant(mt)
        if not E_LATE:
            exps(0)

        n_chunks = 16
        dq_g = [lambda it=it, e=DQ_ENG[k]: interleave(e, *it) for k, it in enumerate(dq)]
        dq_v = [lambda it=it: quant_w(*it) for it in dq]
        for k in range(DQ_AT):
            dq_g.pop(0)()
        z2(0)
        for k, grp in enumerate(GROUPS):
            mine = [i for r in grp for i in (2 * r, 2 * r + 1)]
            nxt = []
            if k + 1 < len(GROUPS):
                ng = GROUPS[k + 1]
                for r in ng:
                    if r % 2 == 0:
                        for mt in range(max(r, X_EARLY), r + 2):
                            nxt.append((256, lambda mt=mt: (x_turn(mt), x_quant(mt))))
                    for j in range(2):
                        nxt.append((512, lambda r=r, j=j: squares(r, j)))
                for r in ([0] if k == 0 and E_LATE else []) + ng:
                    nxt.append((1024, lambda r=r: exps(r)))
                for r in ng:
                    nxt.append((1024, lambda r=r: rsq(r)))
                for r in ng:
                    for ml in range(2):
                        nxt.append((1024, lambda r=r, ml=ml: sines(r, ml)))
            total = sum(c for c, _ in nxt)
            done = 0
            for n, i in enumerate(mine):
                weigh(i)
                products(i)
                if i + 1 < n_chunks:
                    nz = lambda i=i: z2(i + 1)
                    nz()
                turn(i)
                while nxt and done < total * (n + 1) / len(mine) - 1:
                    c, fn = nxt.pop(0)
                    done += c
                    fn()
                if i >= 1:
                    u(i - 1)
                if i >= 2:
                    uquant(i - 2)
                for _ in range(2):
                    if dq_g:
                        dq_g.pop(0)()
                    if dq_v and len(dq_g) < len(dq_v) - 1 or dq_v and not dq_g:
                        dq_v.pop(0)()
                for lag, fn in ((LAG_D, decode), (LAG_D + 1, cast), (LAG_D + 2, planes_turn), (LAG_D + 3, planes_quant)):
                    a = i - lag
                    if a >= 0 and (a // 2) % 2 == 1:
                        fn(place(a)[2])
        u(15)
        uquant(14)
        uquant(15)
        for a in range(16, 16 + LAG_D + 3):
            for lag, fn in ((LAG_D, decode), (LAG_D + 1, cast), (LAG_D + 2, planes_turn), (LAG_D + 3, planes_quant)):
                c = a - lag
                if 0 <= c < 16 and (c // 2) % 2 == 1:
                    fn(place(c)[2])
        for q in range(4):
            nc.sync.dma_start(
                out=out_2[:, 4 * q : 4 * q + 4, :].rearrange("g r m -> r g m").bitcast(I32),
                in_=planes_s[32 * q : 32 * q + 4, :, :].bitcast(I32),
            )
